import numpy as np
import ml_dtypes


def mxq(x, axis, fmt="e4m3"):
    dtype, down = {"e4m3": (ml_dtypes.float8_e4m3fn, 7), "e5m2": (ml_dtypes.float8_e5m2, 14)}[fmt]
    v = np.moveaxis(np.asarray(x, np.float32).astype(ml_dtypes.bfloat16).astype(np.float64), axis, -1)
    blocks = v.reshape(v.shape[:-1] + (-1, 32))
    amax = np.abs(blocks).max(-1, keepdims=True)
    byte = np.maximum(np.where(amax > 0, np.frexp(amax)[1] - 1 + 127, 0) - down, 1)
    scale = np.exp2(byte - 127.0)
    codes = (blocks / scale).astype(np.float32).astype(dtype).astype(np.float64)
    return np.moveaxis((codes * scale).reshape(v.shape), -1, axis)


WIDE = False


def mx_kscale(k):
    if not WIDE:
        return np.ones(k)
    levels = np.array([10, -10, 5, -5, 0])
    if k % 512:
        return np.exp2(np.random.permutation(np.resize(levels, k // 32))).repeat(32)
    a = np.empty((k // 512, 16))
    for p in range(k // 512):
        a[p, :8] = np.random.permutation(np.resize(levels, 8))
        for g in range(8):
            far = levels[np.abs(levels - a[p, g]) >= 10]
            a[p, g + 8] = far[np.random.randint(len(far))]
    return np.exp2(a.ravel()).repeat(32)


def f64(x):
    return np.asarray(x).astype(np.float64)


def striped8(idx):
    return np.asarray(idx).reshape(8, -1, 16).transpose(0, 2, 1).reshape(128, -1).astype(np.uint16)


def unstriped8(offs):
    return offs.reshape(8, 16, -1).transpose(0, 2, 1).reshape(8, -1).astype(np.int64)


def pick8(x, idx, run):
    r = np.arange(len(x))
    return x[r[:, None], idx[r % (8 * run) // run]]


E2M1 = np.array([0.0, 0.5, 1.0, 1.5, 2.0, 3.0, 4.0, 6.0, -0.0, -0.5, -1.0, -1.5, -2.0, -3.0, -4.0, -6.0])


def pack_weight(w, fmt):
    k, n = w.shape
    w = f64(np.asarray(w, np.float32).astype(ml_dtypes.bfloat16)).reshape(k // 32, 32, n)
    amax = np.abs(w).max(1)
    if fmt == "e4m3":
        byte = np.frexp(amax)[1] - 1 + 127 - 7
    else:
        mant, ex = np.frexp(amax / 6.0)
        byte = np.where(mant > 0.5, ex, ex - 1) + 127
    byte = np.clip(np.where(amax > 0, byte, 1), 1, 254)
    scaled = (w * np.exp2(127.0 - byte)[:, None, :]).reshape(k, n).astype(np.float32)
    by_word = np.ascontiguousarray(scaled.reshape(k // 512, 128, 4, n).transpose(0, 1, 3, 2))
    if fmt == "e4m3":
        words = by_word.astype(ml_dtypes.float8_e4m3fn).view(np.uint8)
    else:
        c = by_word.astype(ml_dtypes.float4_e2m1fn).view(np.uint8) & 0xF
        words = (c[..., 0::2] | (c[..., 1::2] << 4)).reshape(k // 512, 128, 2 * n)
    return np.ascontiguousarray(words), np.ascontiguousarray(byte.astype(np.uint8).reshape(k // 512, 16, n))


def unpack_weight(words, scales, fmt):
    g, _, n = scales.shape
    words = np.ascontiguousarray(words).reshape(g, 128, n, -1)
    if fmt == "e4m3":
        vals = words.view(ml_dtypes.float8_e4m3fn).astype(np.float64)
    else:
        nib = np.empty((g, 128, n, 4), np.uint8)
        nib[..., 0::2] = words & 0xF
        nib[..., 1::2] = words >> 4
        vals = E2M1[nib]
    vals = vals * np.repeat(np.exp2(scales.astype(np.float64) - 127.0), 8, axis=1)[..., None]
    return vals.transpose(0, 1, 3, 2).reshape(g * 512, n)


D, T, U, X, I, Q = 512, 1024, 1024, 1024, 512, 128


def setup_inputs():
    n = np.random.standard_normal
    idx = np.stack([np.random.permutation(T)[:I] for _ in range(8)])
    idx2 = np.stack([np.random.permutation(X)[:I] for _ in range(8)])
    idx3 = np.stack([np.random.permutation(U)[:I] for _ in range(8)])
    idx4 = np.stack([np.random.permutation(X)[:I] for _ in range(8)])
    idx5 = np.stack([np.random.permutation(X)[:I] for _ in range(8)])
    fd = mx_kscale(D)
    keysp = pack_weight(n((D, T)) / fd[:, None], "e2m1")
    notesp = pack_weight(n((D, U)) / fd[:, None], "e4m3")
    usersp = pack_weight(n((D, X)) / fd[:, None], "e2m1")
    return {
        "query": (n((D, Q)) * 1.0 / np.sqrt(D) * fd[:, None]).astype(np.float32),
        "keys_words": keysp[0],
        "keys_scales": keysp[1],
        "notes_words": notesp[0],
        "notes_scales": notesp[1],
        "users_words": usersp[0],
        "users_scales": usersp[1],
        "offs": striped8(idx),
        "offs2": striped8(idx2),
        "offs3": striped8(idx3),
        "offs4": striped8(idx4),
        "offs5": striped8(idx5),
    }


def reference(query, keys_words, keys_scales, notes_words, notes_scales, users_words, users_scales, offs, offs2, offs3, offs4, offs5):
    idx = unstriped8(offs)
    idx2 = unstriped8(offs2)
    idx3 = unstriped8(offs3)
    idx4 = unstriped8(offs4)
    idx5 = unstriped8(offs5)
    keysu = unpack_weight(keys_words, keys_scales, "e2m1")
    notesu = unpack_weight(notes_words, notes_scales, "e4m3")
    usersu = unpack_weight(users_words, users_scales, "e2m1")
    queryq = mxq(f64(query), 0, "e4m3")
    a = queryq.T @ keysu
    b = queryq.T @ notesu
    c0 = queryq.T @ usersu
    f1 = np.zeros((Q, X))
    f1[np.arange(Q)[:, None], idx2[np.arange(Q) % 128 // 16]] = pick8(a, idx, 16)
    f2 = np.zeros((Q, X))
    f2[np.arange(Q)[:, None], idx4[np.arange(Q) % 128 // 16]] = pick8(b, idx3, 16)
    r = f1 - f2
    cc = c0 - r
    m1 = np.maximum(cc, f1)
    y = pick8(m1, idx5, 16) + pick8(b, idx3, 16)
    return y

@@ -1,0 +1,129 @@
+from contextlib import ExitStack
+
+import concourse.mybir as mybir
+
+D, T, I, Q = 512, 1024, 512, 128
+FLOPS = 3 * 2 * D * Q * T
+
+F32 = mybir.dt.float32
+BF16 = mybir.dt.bfloat16
+I32 = mybir.dt.int32
+U32 = mybir.dt.uint32
+U16 = mybir.dt.uint16
+U8 = mybir.dt.uint8
+FP8X4 = mybir.dt.float8_e4m3fn_x4
+FP4X4 = mybir.dt.float4_e2m1fn_x4
+ALU = mybir.AluOpType
+COPY = mybir.ActivationFunctionType.Copy
+
+P = 128
+HALF = I // 2
+LH = HALF // 16
+
+
+def tile_attend_balancesheet_three_kernel(tc, query, keys_words, keys_scales, notes_words, notes_scales,
+                                           users_words, users_scales, offs, offs2, offs3, offs4, offs5, out):
+    nc = tc.nc
+    with ExitStack() as ctx:
+        sb = ctx.enter_context(tc.tile_pool(name="sb", bufs=1))
+        ps = ctx.enter_context(tc.psum_pool(name="ps", bufs=1))
+
+        def load_list(src, name):
+            t = sb.tile([P, I // 16], U16, name=name)
+            nc.sync.dma_start(t[:], src)
+            return t
+
+        def zeroed_plane(name):
+            t = sb.tile([P, T], U8, name=name, align_bytes=64)
+            nc.vector.memset(t[:].bitcast(I32), 0)
+            return t
+
+        def load_plane(t, src):
+            for g in range(4):
+                nc.sync.dma_start(t[32 * g : 32 * g + 4, :].bitcast(I32), src[0, 4 * g : 4 * g + 4, :].bitcast(I32))
+
+        ks = zeroed_plane("ks")
+        ns = zeroed_plane("ns")
+        us = zeroed_plane("us")
+        f1 = sb.tile([P, T], F32, name="f1")
+        f2 = sb.tile([P, T], F32, name="f2")
+        nc.vector.memset(f1[:], 0.0)
+        nc.vector.memset(f2[:], 0.0)
+
+        q_raw = sb.tile([P, 4, Q], F32, name="q_raw")
+        nc.sync.dma_start(q_raw[:], query.rearrange("(p j) q -> p j q", j=4))
+        load_plane(ks, keys_scales)
+        kw = sb.tile([P, 2 * T], U8, name="kw", align_bytes=64)
+        nc.sync.dma_start(kw[:].bitcast(I32), keys_words[0].bitcast(I32))
+        l1 = load_list(offs, "l1")
+        nw = sb.tile([P, T], U32, name="nw", align_bytes=64)
+        nc.sync.dma_start(nw[:].bitcast(I32), notes_words[0].rearrange("p n t -> p (n t)").bitcast(I32))
+        l2 = load_list(offs2, "l2")
+        load_plane(ns, notes_scales)
+        l3 = load_list(offs3, "l3")
+        l4 = load_list(offs4, "l4")
+        uw = sb.tile([P, 2 * T], U8, name="uw", align_bytes=64)
+        nc.sync.dma_start(uw[:].bitcast(I32), users_words[0].bitcast(I32))
+        load_plane(us, users_scales)
+        l5 = load_list(offs5, "l5")
+
+        q_bf = sb.tile([P, Q, 4], BF16, name="q_bf", align_bytes=64)
+        nc.vector.tensor_copy(q_bf[:].rearrange("p (c i) t -> p c t i", i=4), q_raw[:].rearrange("p t (c i) -> p c t i", i=4))
+        qw = sb.tile([P, Q], U32, name="qw", align_bytes=64)
+        qs = sb.tile([P, Q], U8, name="qs", align_bytes=64)
+        nc.vector.quantize_mx(qw[:].bitcast(FP8X4), qs[:], q_bf[:].rearrange("p q t -> p (q t)"))
+
+        def product(bank, words, plane):
+            nc.tensor.matmul_mx(bank[:], lhsT=qw[:].bitcast(FP8X4), lhsT_scale=qs[:], rhs=words, rhs_scale=plane, start=True, stop=True)
+
+        a = sb.tile([P, T], F32, name="a")
+        W = 256
+        for j in range(T // W):
+            bank = ps.tile([P, W], F32, name="pa%d" % j)
+            product(bank, kw[:, 2 * W * j : 2 * W * (j + 1)].bitcast(FP4X4), ks[:, W * j : W * (j + 1)])
+            if j % 2 == 0:
+                nc.scalar.copy(a[:, W * j : W * (j + 1)], bank[:])
+            else:
+                nc.vector.tensor_copy(a[:, W * j : W * (j + 1)], bank[:])
+        ga0 = sb.tile([P, HALF], F32, name="ga0")
+        ga1 = sb.tile([P, HALF], F32, name="ga1")
+        nc.vector.tensor_copy(ga0[:], a[:].indirect(l1[:, 0:LH]))
+        nc.scalar.activation(ga1[:], a[:].indirect(l1[:, LH : 2 * LH]), COPY)
+        nc.vector.tensor_copy(f1[:].indirect(l2[:, 0:LH]), ga0[:])
+        nc.vector.tensor_copy(f1[:].indirect(l2[:, LH : 2 * LH]), ga1[:])
+
+        b = sb.tile([P, T], F32, name="b")
+        W = 512
+        for j in range(T // W):
+            bank = ps.tile([P, W], F32, name="pb%d" % j)
+            product(bank, nw[:, W * j : W * (j + 1)].bitcast(FP8X4), ns[:, W * j : W * (j + 1)])
+            nc.scalar.copy(b[:, W * j : W * (j + 1)], bank[:])
+        gb = sb.tile([P, I], F32, name="gb")
+        nc.scalar.activation(gb[:], b[:].indirect(l3[:]), COPY)
+        nc.vector.tensor_copy(f2[:].indirect(l4[:]), gb[:])
+
+        m1 = sb.tile([P, T], F32, name="m1")
+        cc = []
+        for j in range(T // W):
+            cols = slice(W * j, W * (j + 1))
+            bank = ps.tile([P, W], F32, name="pc%d" % j)
+            product(bank, uw[:, 2 * W * j : 2 * W * (j + 1)].bitcast(FP4X4), us[:, cols])
+            c0 = sb.tile([P, W], F32, name="c0_%d" % j)
+            nc.scalar.copy(c0[:], bank[:])
+            g = sb.tile([P, W], F32, name="g%d" % j)
+            nc.gpsimd.tensor_tensor(g[:], c0[:], f1[:, cols], ALU.subtract)
+            c = sb.tile([P, W], F32, name="cc%d" % j)
+            nc.vector.tensor_tensor(c[:], g[:], f2[:, cols], ALU.add)
+            cc.append(c)
+        for j in range(T // W):
+            cols = slice(W * j, W * (j + 1))
+            nc.vector.tensor_tensor(m1[:, cols], cc[j][:], f1[:, cols], ALU.max)
+
+        y0 = sb.tile([P, HALF], F32, name="y0")
+        y1 = sb.tile([P, HALF], F32, name="y1")
+        gm1 = sb.tile([P, HALF], F32, name="gm1")
+        nc.vector.tensor_tensor(y0[:], m1[:].indirect(l5[:, 0:LH]), gb[:, 0:HALF], ALU.add)
+        nc.scalar.activation(gm1[:], m1[:].indirect(l5[:, LH : 2 * LH]), COPY)
+        nc.sync.dma_start(out[:, 0:HALF], y0[:])
+        nc.vector.tensor_tensor(y1[:], gm1[:], gb[:, HALF:I], ALU.add)
+        nc.sync.dma_start(out[:, HALF:I], y1[:])

@@ -46,15 +46,13 @@ def tile_attend_balancesheet_three_kernel(tc, query, keys_words, keys_scales, no
         ns = zeroed_plane("ns")
         us = zeroed_plane("us")
         f1 = sb.tile([P, T], F32, name="f1")
-        f2 = sb.tile([P, T], F32, name="f2")
         nc.vector.memset(f1[:], 0.0)
-        nc.vector.memset(f2[:], 0.0)
 
         q_raw = sb.tile([P, 4, Q], F32, name="q_raw")
         nc.sync.dma_start(q_raw[:], query.rearrange("(p j) q -> p j q", j=4))
-        load_plane(ks, keys_scales)
         kw = sb.tile([P, 2 * T], U8, name="kw", align_bytes=64)
         nc.sync.dma_start(kw[:].bitcast(I32), keys_words[0].bitcast(I32))
+        load_plane(ks, keys_scales)
         l1 = load_list(offs, "l1")
         nw = sb.tile([P, T], U32, name="nw", align_bytes=64)
         nc.sync.dma_start(nw[:].bitcast(I32), notes_words[0].rearrange("p n t -> p (n t)").bitcast(I32))
@@ -67,16 +65,21 @@ def tile_attend_balancesheet_three_kernel(tc, query, keys_words, keys_scales, no
         load_plane(us, users_scales)
         l5 = load_list(offs5, "l5")
 
-        q_bf = sb.tile([P, Q, 4], BF16, name="q_bf", align_bytes=64)
-        nc.vector.tensor_copy(q_bf[:].rearrange("p (c i) t -> p c t i", i=4), q_raw[:].rearrange("p t (c i) -> p c t i", i=4))
+        q_bf = sb.tile([P, Q, 4], BF16, name="q_bf", tag="f2", align_bytes=64)
+        halves = [slice(0, Q // 2), slice(Q // 2, Q)]
+        for rows in halves:
+            nc.vector.tensor_copy(q_bf[:, rows, :].rearrange("p (c i) t -> p c t i", i=4), q_raw[:, :, rows].rearrange("p t (c i) -> p c t i", i=4))
         qw = sb.tile([P, Q], U32, name="qw", align_bytes=64)
         qs = sb.tile([P, Q], U8, name="qs", align_bytes=64)
-        nc.vector.quantize_mx(qw[:].bitcast(FP8X4), qs[:], q_bf[:].rearrange("p q t -> p (q t)"))
+        for rows in halves:
+            nc.vector.quantize_mx(qw[:, rows].bitcast(FP8X4), qs[:, rows], q_bf[:, rows, :].rearrange("p q t -> p (q t)"))
+        f2 = sb.tile([P, T], F32, name="f2", tag="f2", align_bytes=64)
+        nc.vector.memset(f2[:], 0.0)
 
         def product(bank, words, plane):
             nc.tensor.matmul_mx(bank[:], lhsT=qw[:].bitcast(FP8X4), lhsT_scale=qs[:], rhs=words, rhs_scale=plane, start=True, stop=True)
 
-        a = sb.tile([P, T], F32, name="a")
+        a = sb.tile([P, T], F32, name="a", tag="scores")
         W = 256
         for j in range(T // W):
             bank = ps.tile([P, W], F32, name="pa%d" % j)
@@ -85,14 +88,12 @@ def tile_attend_balancesheet_three_kernel(tc, query, keys_words, keys_scales, no
                 nc.scalar.copy(a[:, W * j : W * (j + 1)], bank[:])
             else:
                 nc.vector.tensor_copy(a[:, W * j : W * (j + 1)], bank[:])
-        ga0 = sb.tile([P, HALF], F32, name="ga0")
-        ga1 = sb.tile([P, HALF], F32, name="ga1")
-        nc.vector.tensor_copy(ga0[:], a[:].indirect(l1[:, 0:LH]))
-        nc.scalar.activation(ga1[:], a[:].indirect(l1[:, LH : 2 * LH]), COPY)
-        nc.vector.tensor_copy(f1[:].indirect(l2[:, 0:LH]), ga0[:])
-        nc.vector.tensor_copy(f1[:].indirect(l2[:, LH : 2 * LH]), ga1[:])
+        ga = sb.tile([P, I], F32, name="ga")
+        nc.vector.tensor_copy(ga[:, 0:HALF], a[:].indirect(l1[:, 0:LH]))
+        nc.scalar.activation(ga[:, HALF:I], a[:].indirect(l1[:, LH : 2 * LH]), COPY)
+        nc.vector.tensor_copy(f1[:].indirect(l2[:]), ga[:])
 
-        b = sb.tile([P, T], F32, name="b")
+        b = sb.tile([P, T], F32, name="b", tag="scores")
         W = 512
         for j in range(T // W):
             bank = ps.tile([P, W], F32, name="pb%d" % j)
@@ -104,14 +105,14 @@ def tile_attend_balancesheet_three_kernel(tc, query, keys_words, keys_scales, no
 
         m1 = sb.tile([P, T], F32, name="m1")
         cc = []
+        c0 = sb.tile([P, T], F32, name="c0", tag="scores")
         for j in range(T // W):
             cols = slice(W * j, W * (j + 1))
             bank = ps.tile([P, W], F32, name="pc%d" % j)
             product(bank, uw[:, 2 * W * j : 2 * W * (j + 1)].bitcast(FP4X4), us[:, cols])
-            c0 = sb.tile([P, W], F32, name="c0_%d" % j)
-            nc.scalar.copy(c0[:], bank[:])
+            nc.scalar.copy(c0[:, cols], bank[:])
             g = sb.tile([P, W], F32, name="g%d" % j)
-            nc.gpsimd.tensor_tensor(g[:], c0[:], f1[:, cols], ALU.subtract)
+            nc.gpsimd.tensor_tensor(g[:], c0[:, cols], f1[:, cols], ALU.subtract)
             c = sb.tile([P, W], F32, name="cc%d" % j)
             nc.vector.tensor_tensor(c[:], g[:], f2[:, cols], ALU.add)
             cc.append(c)
@@ -119,11 +120,8 @@ def tile_attend_balancesheet_three_kernel(tc, query, keys_words, keys_scales, no
             cols = slice(W * j, W * (j + 1))
             nc.vector.tensor_tensor(m1[:, cols], cc[j][:], f1[:, cols], ALU.max)
 
-        y0 = sb.tile([P, HALF], F32, name="y0")
-        y1 = sb.tile([P, HALF], F32, name="y1")
-        gm1 = sb.tile([P, HALF], F32, name="gm1")
-        nc.vector.tensor_tensor(y0[:], m1[:].indirect(l5[:, 0:LH]), gb[:, 0:HALF], ALU.add)
-        nc.scalar.activation(gm1[:], m1[:].indirect(l5[:, LH : 2 * LH]), COPY)
-        nc.sync.dma_start(out[:, 0:HALF], y0[:])
-        nc.vector.tensor_tensor(y1[:], gm1[:], gb[:, HALF:I], ALU.add)
-        nc.sync.dma_start(out[:, HALF:I], y1[:])
+        for h in range(2):
+            y = sb.tile([P, HALF], F32, name="y%d" % h)
+            slots = slice(HALF * h, HALF * (h + 1))
+            nc.vector.tensor_tensor(y[:], m1[:].indirect(l5[:, LH * h : LH * (h + 1)]), gb[:, slots], ALU.add)
+            nc.sync.dma_start(out[:, slots], y[:])

@@ -1,6 +1,7 @@
 from contextlib import ExitStack
 
 import concourse.mybir as mybir
+from concourse.masks import make_identity
 
 D, T, I, Q = 512, 1024, 512, 128
 FLOPS = 3 * 2 * D * Q * T
@@ -82,7 +83,7 @@ def tile_attend_balancesheet_three_kernel(tc, query, keys_words, keys_scales, no
         a = sb.tile([P, T], F32, name="a", tag="scores")
         W = 256
         for j in range(T // W):
-            bank = ps.tile([P, W], F32, name="pa%d" % j)
+            bank = ps.tile([P, W], F32, name="pa%d" % j, tag="bank%d" % j)
             product(bank, kw[:, 2 * W * j : 2 * W * (j + 1)].bitcast(FP4X4), ks[:, W * j : W * (j + 1)])
             if j % 2 == 0:
                 nc.scalar.copy(a[:, W * j : W * (j + 1)], bank[:])
@@ -103,22 +104,37 @@ def tile_attend_balancesheet_three_kernel(tc, query, keys_words, keys_scales, no
         nc.scalar.activation(gb[:], b[:].indirect(l3[:]), COPY)
         nc.vector.tensor_copy(f2[:].indirect(l4[:]), gb[:])
 
+        ident = sb.tile([P, P], F32, name="ident")
+        make_identity(nc, ident[:])
+        blocks = [slice(P * r, P * (r + 1)) for r in range(W // P)]
+        lo, hi = slice(0, W), slice(W, T)
+        bank = ps.tile([P, W], F32, name="pct", tag="turn")
+        for r, blk in enumerate(blocks):
+            nc.tensor.matmul_mx(bank[:, blk], lhsT=uw[:, 2 * P * r : 2 * P * (r + 1)].bitcast(FP4X4), lhsT_scale=us[:, blk],
+                                rhs=qw[:].bitcast(FP8X4), rhs_scale=qs[:], start=True, stop=True)
+        c0t = sb.tile([P, W], F32, name="c0t", tag="scores")
+        nc.scalar.copy(c0t[:], bank[:])
+        c0_hi = ps.tile([P, W], F32, name="c0_hi")
+        product(c0_hi, uw[:, 2 * W : 2 * T].bitcast(FP4X4), us[:, hi])
+        bank = ps.tile([P, W], F32, name="px", tag="turn")
+        for blk in blocks:
+            nc.tensor.transpose(bank[:, blk], f1[:, blk], ident[:])
+        nf1t = sb.tile([P, W], F32, name="nf1t", tag="nf1t")
+        nc.scalar.activation(nf1t[:], bank[:], COPY, scale=-1.0)
+        g_lo = ps.tile([P, W], F32, name="g_lo", tag="bank0")
+        for r, blk in enumerate(blocks):
+            nc.tensor.matmul(g_lo[:, blk], lhsT=c0t[:, blk], rhs=ident[:], is_transpose=True, start=(r == 0), stop=False)
+        for r, blk in enumerate(blocks):
+            nc.tensor.matmul(g_lo[:, blk], lhsT=nf1t[:, blk], rhs=ident[:], is_transpose=True, start=False, stop=(r == len(blocks) - 1))
+        g_hi = sb.tile([P, W], F32, name="g_hi")
+        nc.vector.tensor_tensor(g_hi[:], c0_hi[:], f1[:, hi], ALU.subtract)
+        cc_lo = sb.tile([P, W], F32, name="cc_lo")
+        cc_hi = sb.tile([P, W], F32, name="cc_hi", tag="nf1t")
         m1 = sb.tile([P, T], F32, name="m1")
-        cc = []
-        c0 = sb.tile([P, T], F32, name="c0", tag="scores")
-        for j in range(T // W):
-            cols = slice(W * j, W * (j + 1))
-            bank = ps.tile([P, W], F32, name="pc%d" % j)
-            product(bank, uw[:, 2 * W * j : 2 * W * (j + 1)].bitcast(FP4X4), us[:, cols])
-            nc.scalar.copy(c0[:, cols], bank[:])
-            g = sb.tile([P, W], F32, name="g%d" % j)
-            nc.gpsimd.tensor_tensor(g[:], c0[:, cols], f1[:, cols], ALU.subtract)
-            c = sb.tile([P, W], F32, name="cc%d" % j)
-            nc.vector.tensor_tensor(c[:], g[:], f2[:, cols], ALU.add)
-            cc.append(c)
-        for j in range(T // W):
-            cols = slice(W * j, W * (j + 1))
-            nc.vector.tensor_tensor(m1[:, cols], cc[j][:], f1[:, cols], ALU.max)
+        nc.vector.tensor_tensor(cc_lo[:], g_lo[:], f2[:, lo], ALU.add)
+        nc.vector.tensor_tensor(cc_hi[:], g_hi[:], f2[:, hi], ALU.add)
+        nc.vector.tensor_tensor(m1[:, lo], cc_lo[:], f1[:, lo], ALU.max)
+        nc.vector.tensor_tensor(m1[:, hi], cc_hi[:], f1[:, hi], ALU.max)
 
         for h in range(2):
             y = sb.tile([P, HALF], F32, name="y%d" % h)

@@ -89,7 +89,7 @@ def tile_attend_balancesheet_three_kernel(tc, query, keys_words, keys_scales, no
                 nc.scalar.copy(a[:, W * j : W * (j + 1)], bank[:])
             else:
                 nc.vector.tensor_copy(a[:, W * j : W * (j + 1)], bank[:])
-        ga = sb.tile([P, I], F32, name="ga")
+        ga = sb.tile([P, I], F32, name="ga", tag="ga")
         nc.vector.tensor_copy(ga[:, 0:HALF], a[:].indirect(l1[:, 0:LH]))
         nc.scalar.activation(ga[:, HALF:I], a[:].indirect(l1[:, LH : 2 * LH]), COPY)
         nc.vector.tensor_copy(f1[:].indirect(l2[:]), ga[:])
@@ -113,27 +113,35 @@ def tile_attend_balancesheet_three_kernel(tc, query, keys_words, keys_scales, no
             nc.tensor.matmul_mx(bank[:, blk], lhsT=uw[:, 2 * P * r : 2 * P * (r + 1)].bitcast(FP4X4), lhsT_scale=us[:, blk],
                                 rhs=qw[:].bitcast(FP8X4), rhs_scale=qs[:], start=True, stop=True)
         c0t = sb.tile([P, W], F32, name="c0t", tag="scores")
-        nc.scalar.copy(c0t[:], bank[:])
-        c0_hi = ps.tile([P, W], F32, name="c0_hi")
-        product(c0_hi, uw[:, 2 * W : 2 * T].bitcast(FP4X4), us[:, hi])
+        nc.scalar.activation(c0t[:], bank[:], COPY, scale=-1.0)
+        bank = ps.tile([P, W], F32, name="pch", tag="bank1")
+        product(bank, uw[:, 2 * W : 2 * T].bitcast(FP4X4), us[:, hi])
+        c0_hi = sb.tile([P, W], F32, name="c0_hi", tag="ga")
+        nc.scalar.copy(c0_hi[:], bank[:])
+        g_hi = sb.tile([P, W], F32, name="g_hi")
+        nc.gpsimd.tensor_tensor(g_hi[:], c0_hi[:], f1[:, hi], ALU.subtract)
         bank = ps.tile([P, W], F32, name="px", tag="turn")
         for blk in blocks:
             nc.tensor.transpose(bank[:, blk], f1[:, blk], ident[:])
         nf1t = sb.tile([P, W], F32, name="nf1t", tag="nf1t")
-        nc.scalar.activation(nf1t[:], bank[:], COPY, scale=-1.0)
+        nc.scalar.copy(nf1t[:], bank[:])
         g_lo = ps.tile([P, W], F32, name="g_lo", tag="bank0")
         for r, blk in enumerate(blocks):
             nc.tensor.matmul(g_lo[:, blk], lhsT=c0t[:, blk], rhs=ident[:], is_transpose=True, start=(r == 0), stop=False)
         for r, blk in enumerate(blocks):
             nc.tensor.matmul(g_lo[:, blk], lhsT=nf1t[:, blk], rhs=ident[:], is_transpose=True, start=False, stop=(r == len(blocks) - 1))
-        g_hi = sb.tile([P, W], F32, name="g_hi")
-        nc.vector.tensor_tensor(g_hi[:], c0_hi[:], f1[:, hi], ALU.subtract)
+        f1_lo = ps.tile([P, W], F32, name="f1_lo", tag="bank2")
+        for blk in blocks:
+            nc.tensor.transpose(f1_lo[:, blk], nf1t[:, blk], ident[:])
         cc_lo = sb.tile([P, W], F32, name="cc_lo")
-        cc_hi = sb.tile([P, W], F32, name="cc_hi", tag="nf1t")
-        m1 = sb.tile([P, T], F32, name="m1")
-        nc.vector.tensor_tensor(cc_lo[:], g_lo[:], f2[:, lo], ALU.add)
-        nc.vector.tensor_tensor(cc_hi[:], g_hi[:], f2[:, hi], ALU.add)
-        nc.vector.tensor_tensor(m1[:, lo], cc_lo[:], f1[:, lo], ALU.max)
+        cc_hi = sb.tile([P, W], F32, name="cc_hi")
+        m1 = sb.tile([P, T], F32, name="m1", tag="nf1t")
+        nc.gpsimd.tensor_tensor(cc_hi[:], g_hi[:], f2[:, hi], ALU.add)
+        quarters = [slice(0, W // 2), slice(W // 2, W)]
+        for cols in quarters:
+            nc.vector.tensor_tensor(cc_lo[:, cols], f2[:, cols], g_lo[:, cols], ALU.subtract)
+        for cols in quarters:
+            nc.vector.tensor_tensor(m1[:, cols], cc_lo[:, cols], f1_lo[:, cols], ALU.max)
         nc.vector.tensor_tensor(m1[:, hi], cc_hi[:], f1[:, hi], ALU.max)
 
         for h in range(2):

from contextlib import ExitStack

import concourse.mybir as mybir
from concourse.masks import make_identity

D, T, I, Q = 512, 1024, 512, 128
FLOPS = 3 * 2 * D * Q * T

F32 = mybir.dt.float32
BF16 = mybir.dt.bfloat16
I32 = mybir.dt.int32
U32 = mybir.dt.uint32
U16 = mybir.dt.uint16
U8 = mybir.dt.uint8
FP8X4 = mybir.dt.float8_e4m3fn_x4
FP4X4 = mybir.dt.float4_e2m1fn_x4
ALU = mybir.AluOpType
COPY = mybir.ActivationFunctionType.Copy

P = 128
HALF = I // 2
LH = HALF // 16


def tile_attend_balancesheet_three_kernel(tc, query, keys_words, keys_scales, notes_words, notes_scales,
                                           users_words, users_scales, offs, offs2, offs3, offs4, offs5, out):
    nc = tc.nc
    with ExitStack() as ctx:
        sb = ctx.enter_context(tc.tile_pool(name="sb", bufs=1))
        ps = ctx.enter_context(tc.psum_pool(name="ps", bufs=1))

        def load_list(src, name):
            t = sb.tile([P, I // 16], U16, name=name)
            nc.sync.dma_start(t[:], src)
            return t

        def zeroed_plane(name):
            t = sb.tile([P, T], U8, name=name, align_bytes=64)
            nc.vector.memset(t[:].bitcast(I32), 0)
            return t

        def load_plane(t, src):
            for g in range(4):
                nc.sync.dma_start(t[32 * g : 32 * g + 4, :].bitcast(I32), src[0, 4 * g : 4 * g + 4, :].bitcast(I32))

        ks = zeroed_plane("ks")
        ns = zeroed_plane("ns")
        us = zeroed_plane("us")
        f1 = sb.tile([P, T], F32, name="f1")
        nc.vector.memset(f1[:], 0.0)

        q_raw = sb.tile([P, 4, Q], F32, name="q_raw")
        nc.sync.dma_start(q_raw[:], query.rearrange("(p j) q -> p j q", j=4))
        kw = sb.tile([P, 2 * T], U8, name="kw", align_bytes=64)
        nc.sync.dma_start(kw[:].bitcast(I32), keys_words[0].bitcast(I32))
        load_plane(ks, keys_scales)
        l1 = load_list(offs, "l1")
        nw = sb.tile([P, T], U32, name="nw", align_bytes=64)
        nc.sync.dma_start(nw[:].bitcast(I32), notes_words[0].rearrange("p n t -> p (n t)").bitcast(I32))
        l2 = load_list(offs2, "l2")
        load_plane(ns, notes_scales)
        l3 = load_list(offs3, "l3")
        l4 = load_list(offs4, "l4")
        uw = sb.tile([P, 2 * T], U8, name="uw", align_bytes=64)
        nc.sync.dma_start(uw[:].bitcast(I32), users_words[0].bitcast(I32))
        load_plane(us, users_scales)
        l5 = load_list(offs5, "l5")

        q_bf = sb.tile([P, Q, 4], BF16, name="q_bf", tag="f2", align_bytes=64)
        halves = [slice(0, Q // 2), slice(Q // 2, Q)]
        for rows in halves:
            nc.vector.tensor_copy(q_bf[:, rows, :].rearrange("p (c i) t -> p c t i", i=4), q_raw[:, :, rows].rearrange("p t (c i) -> p c t i", i=4))
        qw = sb.tile([P, Q], U32, name="qw", align_bytes=64)
        qs = sb.tile([P, Q], U8, name="qs", align_bytes=64)
        for rows in halves:
            nc.vector.quantize_mx(qw[:, rows].bitcast(FP8X4), qs[:, rows], q_bf[:, rows, :].rearrange("p q t -> p (q t)"))
        f2 = sb.tile([P, T], F32, name="f2", tag="f2", align_bytes=64)
        nc.vector.memset(f2[:], 0.0)

        def product(bank, words, plane):
            nc.tensor.matmul_mx(bank[:], lhsT=qw[:].bitcast(FP8X4), lhsT_scale=qs[:], rhs=words, rhs_scale=plane, start=True, stop=True)

        a = sb.tile([P, T], F32, name="a", tag="scores")
        W = 256
        for j in range(T // W):
            bank = ps.tile([P, W], F32, name="pa%d" % j, tag="bank%d" % j)
            product(bank, kw[:, 2 * W * j : 2 * W * (j + 1)].bitcast(FP4X4), ks[:, W * j : W * (j + 1)])
            if j % 2 == 0:
                nc.scalar.copy(a[:, W * j : W * (j + 1)], bank[:])
            else:
                nc.vector.tensor_copy(a[:, W * j : W * (j + 1)], bank[:])
        ga = sb.tile([P, I], F32, name="ga", tag="ga")
        nc.vector.tensor_copy(ga[:, 0:HALF], a[:].indirect(l1[:, 0:LH]))
        nc.scalar.activation(ga[:, HALF:I], a[:].indirect(l1[:, LH : 2 * LH]), COPY)
        nc.vector.tensor_copy(f1[:].indirect(l2[:]), ga[:])

        b = sb.tile([P, T], F32, name="b", tag="scores")
        W = 512
        for j in range(T // W):
            bank = ps.tile([P, W], F32, name="pb%d" % j)
            product(bank, nw[:, W * j : W * (j + 1)].bitcast(FP8X4), ns[:, W * j : W * (j + 1)])
            nc.scalar.copy(b[:, W * j : W * (j + 1)], bank[:])
        gb = sb.tile([P, I], F32, name="gb")
        nc.scalar.activation(gb[:], b[:].indirect(l3[:]), COPY)
        nc.vector.tensor_copy(f2[:].indirect(l4[:]), gb[:])

        ident = sb.tile([P, P], F32, name="ident")
        make_identity(nc, ident[:])
        blocks = [slice(P * r, P * (r + 1)) for r in range(W // P)]
        lo, hi = slice(0, W), slice(W, T)
        bank = ps.tile([P, W], F32, name="pct", tag="turn")
        for r, blk in enumerate(blocks):
            nc.tensor.matmul_mx(bank[:, blk], lhsT=uw[:, 2 * P * r : 2 * P * (r + 1)].bitcast(FP4X4), lhsT_scale=us[:, blk],
                                rhs=qw[:].bitcast(FP8X4), rhs_scale=qs[:], start=True, stop=True)
        c0t = sb.tile([P, W], F32, name="c0t", tag="scores")
        nc.scalar.activation(c0t[:], bank[:], COPY, scale=-1.0)
        bank = ps.tile([P, W], F32, name="pch", tag="bank1")
        product(bank, uw[:, 2 * W : 2 * T].bitcast(FP4X4), us[:, hi])
        c0_hi = sb.tile([P, W], F32, name="c0_hi", tag="ga")
        nc.scalar.copy(c0_hi[:], bank[:])
        g_hi = sb.tile([P, W], F32, name="g_hi")
        nc.gpsimd.tensor_tensor(g_hi[:], c0_hi[:], f1[:, hi], ALU.subtract)
        bank = ps.tile([P, W], F32, name="px", tag="turn")
        for blk in blocks:
            nc.tensor.transpose(bank[:, blk], f1[:, blk], ident[:])
        nf1t = sb.tile([P, W], F32, name="nf1t", tag="nf1t")
        nc.scalar.copy(nf1t[:], bank[:])
        g_lo = ps.tile([P, W], F32, name="g_lo", tag="bank0")
        for r, blk in enumerate(blocks):
            nc.tensor.matmul(g_lo[:, blk], lhsT=c0t[:, blk], rhs=ident[:], is_transpose=True, start=(r == 0), stop=False)
        for r, blk in enumerate(blocks):
            nc.tensor.matmul(g_lo[:, blk], lhsT=nf1t[:, blk], rhs=ident[:], is_transpose=True, start=False, stop=(r == len(blocks) - 1))
        f1_lo = ps.tile([P, W], F32, name="f1_lo", tag="bank2")
        for blk in blocks:
            nc.tensor.transpose(f1_lo[:, blk], nf1t[:, blk], ident[:])
        cc_lo = sb.tile([P, W], F32, name="cc_lo")
        cc_hi = sb.tile([P, W], F32, name="cc_hi")
        m1 = sb.tile([P, T], F32, name="m1", tag="nf1t")
        nc.gpsimd.tensor_tensor(cc_hi[:], g_hi[:], f2[:, hi], ALU.add)
        quarters = [slice(0, W // 2), slice(W // 2, W)]
        for cols in quarters:
            nc.vector.tensor_tensor(cc_lo[:, cols], f2[:, cols], g_lo[:, cols], ALU.subtract)
        for cols in quarters:
            nc.vector.tensor_tensor(m1[:, cols], cc_lo[:, cols], f1_lo[:, cols], ALU.max)
        nc.vector.tensor_tensor(m1[:, hi], cc_hi[:], f1[:, hi], ALU.max)

        for h in range(2):
            y = sb.tile([P, HALF], F32, name="y%d" % h)
            slots = slice(HALF * h, HALF * (h + 1))
            nc.vector.tensor_tensor(y[:], m1[:].indirect(l5[:, LH * h : LH * (h + 1)]), gb[:, slots], ALU.add)
            nc.sync.dma_start(out[:, slots], y[:])
